import numpy as np
import ml_dtypes


def mxq(x, axis, fmt="e4m3"):
    dtype, down = {"e4m3": (ml_dtypes.float8_e4m3fn, 7), "e5m2": (ml_dtypes.float8_e5m2, 14)}[fmt]
    v = np.moveaxis(np.asarray(x, np.float32).astype(ml_dtypes.bfloat16).astype(np.float64), axis, -1)
    blocks = v.reshape(v.shape[:-1] + (-1, 32))
    amax = np.abs(blocks).max(-1, keepdims=True)
    byte = np.maximum(np.where(amax > 0, np.frexp(amax)[1] - 1 + 127, 0) - down, 1)
    scale = np.exp2(byte - 127.0)
    codes = (blocks / scale).astype(np.float32).astype(dtype).astype(np.float64)
    return np.moveaxis((codes * scale).reshape(v.shape), -1, axis)


WIDE = False


def mx_kscale(k):
    if not WIDE:
        return np.ones(k)
    levels = np.array([10, -10, 5, -5, 0])
    if k % 512:
        return np.exp2(np.random.permutation(np.resize(levels, k // 32))).repeat(32)
    a = np.empty((k // 512, 16))
    for p in range(k // 512):
        a[p, :8] = np.random.permutation(np.resize(levels, 8))
        for g in range(8):
            far = levels[np.abs(levels - a[p, g]) >= 10]
            a[p, g + 8] = far[np.random.randint(len(far))]
    return np.exp2(a.ravel()).repeat(32)


def f64(x):
    return np.asarray(x).astype(np.float64)


def striped8(idx):
    return np.concatenate([x.reshape(-1, 16).T for x in idx]).astype(np.uint16)


def runs(offs, k):
    lists = np.stack([offs[16 * r : 16 * r + 16].T.reshape(-1) for r in range(8)]).astype(np.int64)
    return lists[np.arange(k) % 512 // 64]


def pack_weight(w):
    k, n = w.shape
    w = f64(np.asarray(w, np.float32).astype(ml_dtypes.bfloat16)).reshape(k // 32, 32, n)
    amax = np.abs(w).max(1)
    byte = np.clip(np.where(amax > 0, np.frexp(amax)[1] - 1 + 127 - 7, 1), 1, 254)
    scaled = (w * np.exp2(127.0 - byte)[:, None, :]).reshape(k, n).astype(np.float32)
    words = np.ascontiguousarray(scaled.reshape(k // 512, 128, 4, n).transpose(0, 1, 3, 2)).astype(ml_dtypes.float8_e4m3fn).view(np.uint8)
    return words, np.ascontiguousarray(byte.astype(np.uint8).reshape(k // 512, 16, n))


def unpack_weight(words, scales):
    g, p, n, _ = words.shape
    vals = np.ascontiguousarray(words).view(ml_dtypes.float8_e4m3fn).astype(np.float64) * np.repeat(np.exp2(scales.astype(np.float64) - 127.0), 8, axis=1)[..., None]
    return vals.transpose(0, 1, 3, 2).reshape(g * 512, n)


E2M1 = np.array([0.0, 0.5, 1.0, 1.5, 2.0, 3.0, 4.0, 6.0, -0.0, -0.5, -1.0, -1.5, -2.0, -3.0, -4.0, -6.0])


def pack_fp4(w):
    k, n = w.shape
    w = f64(np.asarray(w, np.float32).astype(ml_dtypes.bfloat16)).reshape(k // 32, 32, n)
    amax = np.abs(w).max(1)
    mant, ex = np.frexp(amax / 6.0)
    byte = np.clip(np.where(amax > 0, np.where(mant > 0.5, ex, ex - 1) + 127, 1), 1, 254)
    scaled = (w * np.exp2(127.0 - byte)[:, None, :]).reshape(k, n).astype(np.float32)
    c = np.ascontiguousarray(scaled.reshape(k // 512, 128, 4, n).transpose(0, 1, 3, 2)).astype(ml_dtypes.float4_e2m1fn).view(np.uint8) & 0xF
    words = (c[..., 0::2] | (c[..., 1::2] << 4)).reshape(k // 512, 128, 2 * n)
    return np.ascontiguousarray(words), np.ascontiguousarray(byte.astype(np.uint8).reshape(k // 512, 16, n))


def unpack_fp4(words, scales):
    g, _, n = scales.shape
    words = np.ascontiguousarray(words).reshape(g, 128, n, 2)
    nib = np.empty((g, 128, n, 4), np.uint8)
    nib[..., 0::2] = words & 0xF
    nib[..., 1::2] = words >> 4
    vals = E2M1[nib] * np.repeat(np.exp2(scales.astype(np.float64) - 127.0), 8, axis=1)[..., None]
    return vals.transpose(0, 1, 3, 2).reshape(g * 512, n)


def planes(y):
    n, m = y.shape
    v = y.astype(np.float32).astype(ml_dtypes.bfloat16).astype(np.float64).reshape(n // 32, 32, m)
    top = np.abs(v).max(1)
    byte = np.clip(np.where(top > 0, np.frexp(top)[1] - 1 + 127 - 7, 1), 1, 254)
    codes = (v * np.exp2(127.0 - byte)[:, None, :]).reshape(n, m).astype(np.float32).astype(ml_dtypes.float8_e4m3fn).view(np.uint8)
    words = codes.reshape(n // 512, 128, 4, m).transpose(0, 1, 3, 2)
    return np.ascontiguousarray(words), np.ascontiguousarray(byte.astype(np.uint8).reshape(n // 512, 16, m))


K, T, S, V, H = 512, 2048, 512, 512, 512


def setup_inputs():
    n = np.random.standard_normal
    s = mx_kscale(K)[:, None]
    packed_xT = pack_weight(n((K, T)) * s)
    packed_w1 = pack_fp4(n((K, H)) / np.sqrt(K) / s)
    return {
        "x_words": packed_xT[0],
        "x_scales": packed_xT[1],
        "w1_words": packed_w1[0],
        "w1_scales": packed_w1[1],
        "gs": (np.random.uniform(0.5, 1.5, (K, 1)) / s).astype(np.float32),
        "offs": striped8(np.random.randint(0, T, (8, S))),
        "cand": striped8(np.random.randint(0, T, (8, V))),
    }


def reference(x_words, x_scales, w1_words, w1_scales, gs, offs, cand):
    x_cand = unpack_weight(x_words, x_scales)[np.arange(K)[:, None], runs(cand, K)]
    xq = unpack_weight(x_words, x_scales)[np.arange(K)[:, None], runs(offs, K)]
    h = np.tanh(unpack_fp4(w1_words, w1_scales).T @ xq)
    z = f64(gs) * h
    out_0 = 0.0625 * ((x_cand.T @ mxq(z, 0, "e4m3")))
    return (out_0,) + planes(out_0)

@@ -1,0 +1,173 @@
+from contextlib import ExitStack
+
+import concourse.mybir as mybir
+from concourse.masks import make_identity
+
+K, T, S, V, H = 512, 2048, 512, 512, 512
+FLOPS = 2 * K * H * S + 2 * K * V * S
+
+F32 = mybir.dt.float32
+BF16 = mybir.dt.bfloat16
+I32 = mybir.dt.int32
+U32 = mybir.dt.uint32
+U16 = mybir.dt.uint16
+U8 = mybir.dt.uint8
+FP8X4 = mybir.dt.float8_e4m3fn_x4
+FP4X4 = mybir.dt.float4_e2m1fn_x4
+ACT = mybir.ActivationFunctionType
+MULT = mybir.AluOpType.mult
+
+P = 128
+PACK = 4
+CHUNK = 128
+CHUNKS = S // CHUNK
+
+
+def tile_picked_candhash_tanh_po_kernel(
+    tc, x_words, x_scales, w1_words, w1_scales, gs, offs, cand, out_0, out_1, out_2
+):
+    nc = tc.nc
+    with ExitStack() as ctx:
+        keep = ctx.enter_context(tc.tile_pool(name="keep", bufs=1))
+        shared = ctx.enter_context(tc.tile_pool(name="shared", bufs=1))
+        psum_a = ctx.enter_context(tc.psum_pool(name="psum_a", bufs=4))
+        psum_t = ctx.enter_context(tc.psum_pool(name="psum_t", bufs=4))
+
+        offs_t = keep.tile([P, S // 16], U16, name="offs_t")
+        cand_t = keep.tile([P, V // 16], U16, name="cand_t")
+        xw = keep.tile([P, T], U32, name="xw", align_bytes=64)
+        xs = shared.tile([P, T], U8, name="xs", align_bytes=64, offset=1024)
+        w1w = keep.tile([P, 2 * H], U8, name="w1w", align_bytes=64)
+        w1s = keep.tile([P, H], U8, name="w1s", align_bytes=64)
+        gs_t = keep.tile([P, PACK], F32, name="gs_t", align_bytes=64)
+        q_words = shared.tile([P, S], U32, name="q_words", align_bytes=64, offset=0)
+        q_raw = keep.tile([P, S], U8, name="q_raw", align_bytes=64)
+        q_plane = keep.tile([P, S], U8, name="q_plane", align_bytes=64)
+        c_words_raw = shared.tile([P, V], U32, name="c_words_raw", align_bytes=64, offset=2048)
+        c_words = keep.tile([P, V], U32, name="c_words", align_bytes=64)
+        c_raw = keep.tile([P, V], U8, name="c_raw", align_bytes=64)
+        c_moved = keep.tile([P, V], U8, name="c_moved", align_bytes=64)
+        c_plane = keep.tile([P, V], U8, name="c_plane", align_bytes=64)
+        ident = keep.tile([P, P], F32, name="ident", align_bytes=64)
+        warm = keep.tile([P, 8], F32, name="warm", align_bytes=64)
+        warm_out = keep.tile([P, 8], F32, name="warm_out", align_bytes=64)
+        o_words = keep.tile([P, S], U32, name="o_words", align_bytes=64)
+        o_scales = keep.tile([P, S], U8, name="o_scales", align_bytes=64)
+
+        nc.vector.memset(xs[:].bitcast(I32), 0)
+        nc.scalar.dma_start(
+            xw[:].bitcast(I32), x_words[0].rearrange("p c r -> p (c r)").bitcast(I32)
+        )
+        nc.sync.dma_start(offs_t[:], offs)
+        nc.sync.dma_start(cand_t[:], cand)
+        nc.sync.dma_start(xs[:].bitcast(I32)[0:P:8, :], x_scales[0].bitcast(I32))
+        nc.sync.dma_start(w1w[:].bitcast(I32), w1_words[0].bitcast(I32))
+        nc.vector.memset(warm[:], 0.0)
+        nc.scalar.activation(warm_out[:], warm[:], ACT.Tanh)
+        nc.vector.memset(w1s[:].bitcast(I32), 0)
+        nc.vector.memset(q_plane[:].bitcast(I32), 0)
+        nc.vector.memset(c_moved[:].bitcast(I32), 0)
+        w1s_rows = w1_scales[0].bitcast(I32)
+        for q in range(4):
+            nc.scalar.dma_start(
+                w1s[:].bitcast(I32)[32 * q : 32 * q + 4, :], w1s_rows[4 * q : 4 * q + 4, :]
+            )
+        make_identity(nc, ident[:])
+
+        def move_rows(dst, src, queue):
+            for r in range(4):
+                queue.dma_start(dst[:].bitcast(I32)[r:P:32, :], src[:].bitcast(I32)[8 * r : P : 32, :])
+
+        nc.vector.tensor_copy(q_raw[:], xs[:].indirect(offs_t[:]))
+        move_rows(q_plane, q_raw, nc.sync)
+        nc.vector.tensor_copy(c_raw[:], xs[:].indirect(cand_t[:]))
+        move_rows(c_moved, c_raw, nc.sync)
+        nc.sync.dma_start(gs_t[:], gs.rearrange("(p t) o -> p (t o)", t=PACK))
+        nc.vector.tensor_copy(q_words[:], xw[:].indirect(offs_t[:]))
+        nc.vector.tensor_copy(c_words_raw[:], xw[:].indirect(cand_t[:]))
+        nc.vector.tensor_copy(
+            c_words[:].bitcast(I32).rearrange("p (t m) -> p m t", t=PACK),
+            c_words_raw[:].bitcast(I32).rearrange("p (m t) -> p m t", t=PACK),
+        )
+        nc.vector.tensor_copy(
+            c_plane[:].rearrange("p (t m) -> p t m", t=PACK),
+            c_moved[:].rearrange("p (m t) -> p t m", t=PACK),
+        )
+
+        cols = [slice(c * CHUNK, (c + 1) * CHUNK) for c in range(CHUNKS)]
+        out_rows = out_0.rearrange("(p t) j -> p t j", t=PACK)
+        out_words = out_1[0].rearrange("p c r -> p (c r)").bitcast(I32)
+
+        turned = []
+        for c in range(CHUNKS):
+            acc = psum_a.tile([P, H], F32, name="acc", tag="acc")
+            nc.tensor.matmul_mx(
+                out=acc[:],
+                lhsT=q_words[:, cols[c]].bitcast(FP8X4),
+                lhsT_scale=q_plane[:, cols[c]],
+                rhs=w1w[:].bitcast(FP4X4),
+                rhs_scale=w1s[:],
+                start=True,
+                stop=True,
+            )
+            h = keep.tile([P, PACK, P], F32, name="h%d" % c, align_bytes=64)
+            nc.scalar.activation(h[:], acc[:].rearrange("p (m t) -> p t m", t=PACK), ACT.Tanh)
+            tr = psum_t.tile([P, PACK, CHUNK], F32, name="tr", tag="tr")
+            for t in range(PACK):
+                nc.tensor.transpose(tr[:, t, :], h[:, t, :], ident[:])
+            turned.append(tr)
+
+        gs_b = gs_t[:].unsqueeze(1).to_broadcast([P, CHUNK, PACK])
+        z = [keep.tile([P, CHUNK, PACK], BF16, name="z%d" % c, align_bytes=64) for c in range(CHUNKS)]
+        zw = [keep.tile([P, CHUNK], U32, name="zw%d" % c, align_bytes=64) for c in range(CHUNKS)]
+        zs = [keep.tile([P, CHUNK], U8, name="zs%d" % c, align_bytes=64) for c in range(CHUNKS)]
+        o32 = [keep.tile([P, PACK, CHUNK], F32, name="o32_%d" % c, align_bytes=64) for c in range(CHUNKS)]
+        ob = [keep.tile([P, CHUNK, PACK], BF16, name="ob%d" % c, align_bytes=64) for c in range(CHUNKS)]
+
+        def weigh(c):
+            nc.vector.tensor_tensor(z[c][:], turned[c][:].rearrange("p t n -> p n t"), gs_b, MULT)
+
+        def score(c):
+            nc.vector.quantize_mx(
+                out=zw[c][:].bitcast(FP8X4), scales=zs[c][:], in_=z[c][:].rearrange("p n t -> p (n t)")
+            )
+            acc = psum_a.tile([P, PACK, CHUNK], F32, name="acc2", tag="acc")
+            for t in range(PACK):
+                rows = slice(t * P, (t + 1) * P)
+                nc.tensor.matmul_mx(
+                    out=acc[:, t, :],
+                    lhsT=c_words[:, rows].bitcast(FP8X4),
+                    lhsT_scale=c_plane[:, rows],
+                    rhs=zw[c][:].bitcast(FP8X4),
+                    rhs_scale=zs[c][:],
+                    start=True,
+                    stop=True,
+                )
+            nc.scalar.activation(o32[c][:], acc[:], ACT.Copy, scale=0.0625)
+            nc.sync.dma_start(out_rows[:, :, cols[c]], o32[c][:])
+
+        def round_out(c):
+            nc.vector.tensor_copy(ob[c][:], o32[c][:].rearrange("p t n -> p n t"))
+
+        def pack_out(c):
+            nc.vector.quantize_mx(
+                out=o_words[:, cols[c]].bitcast(FP8X4),
+                scales=o_scales[:, cols[c]],
+                in_=ob[c][:].rearrange("p n t -> p (n t)"),
+            )
+            nc.sync.dma_start(out_words[:, cols[c]], o_words[:, cols[c]].bitcast(I32))
+
+        for step in range(CHUNKS + 4):
+            if step < CHUNKS:
+                weigh(step)
+            if 0 <= step - 1 < CHUNKS:
+                score(step - 1)
+            if 0 <= step - 3 < CHUNKS:
+                round_out(step - 3)
+            if 0 <= step - 4 < CHUNKS:
+                pack_out(step - 4)
+
+        scale_rows = out_2[0].bitcast(I32)
+        for q in range(4):
+            queue = nc.sync if q % 2 == 0 else nc.scalar
+            queue.dma_start(scale_rows[4 * q : 4 * q + 4, :], o_scales[:].bitcast(I32)[32 * q : 32 * q + 4, :])

@@ -1,7 +1,6 @@
 from contextlib import ExitStack
 
 import concourse.mybir as mybir
-from concourse.masks import make_identity
 
 K, T, S, V, H = 512, 2048, 512, 512, 512
 FLOPS = 2 * K * H * S + 2 * K * V * S
@@ -31,91 +30,104 @@ def tile_picked_candhash_tanh_po_kernel(
         keep = ctx.enter_context(tc.tile_pool(name="keep", bufs=1))
         shared = ctx.enter_context(tc.tile_pool(name="shared", bufs=1))
         psum_a = ctx.enter_context(tc.psum_pool(name="psum_a", bufs=4))
-        psum_t = ctx.enter_context(tc.psum_pool(name="psum_t", bufs=4))
+        psum_o = ctx.enter_context(tc.psum_pool(name="psum_o", bufs=4))
 
         offs_t = keep.tile([P, S // 16], U16, name="offs_t")
         cand_t = keep.tile([P, V // 16], U16, name="cand_t")
         xw = keep.tile([P, T], U32, name="xw", align_bytes=64)
         xs = shared.tile([P, T], U8, name="xs", align_bytes=64, offset=1024)
         w1w = keep.tile([P, 2 * H], U8, name="w1w", align_bytes=64)
-        w1s = keep.tile([P, H], U8, name="w1s", align_bytes=64)
+        w1s = shared.tile([P, H], U8, name="w1s", align_bytes=64, offset=3072)
         gs_t = keep.tile([P, PACK], F32, name="gs_t", align_bytes=64)
         q_words = shared.tile([P, S], U32, name="q_words", align_bytes=64, offset=0)
+        c_words_raw = shared.tile([P, V], U32, name="c_words_raw", align_bytes=64, offset=2048)
         q_raw = keep.tile([P, S], U8, name="q_raw", align_bytes=64)
         q_plane = keep.tile([P, S], U8, name="q_plane", align_bytes=64)
-        c_words_raw = shared.tile([P, V], U32, name="c_words_raw", align_bytes=64, offset=2048)
-        c_words = keep.tile([P, V], U32, name="c_words", align_bytes=64)
         c_raw = keep.tile([P, V], U8, name="c_raw", align_bytes=64)
-        c_moved = keep.tile([P, V], U8, name="c_moved", align_bytes=64)
+        c_dealt = keep.tile([P, V], U8, name="c_dealt", align_bytes=64)
+        c_words = keep.tile([P, V], U32, name="c_words", align_bytes=64)
         c_plane = keep.tile([P, V], U8, name="c_plane", align_bytes=64)
-        ident = keep.tile([P, P], F32, name="ident", align_bytes=64)
+        w1w_dealt = keep.tile([P, 2 * H], U8, name="w1w_dealt", align_bytes=64)
+        w1s_dealt = keep.tile([P, H], U8, name="w1s_dealt", align_bytes=64)
         warm = keep.tile([P, 8], F32, name="warm", align_bytes=64)
         warm_out = keep.tile([P, 8], F32, name="warm_out", align_bytes=64)
         o_words = keep.tile([P, S], U32, name="o_words", align_bytes=64)
         o_scales = keep.tile([P, S], U8, name="o_scales", align_bytes=64)
 
-        nc.vector.memset(xs[:].bitcast(I32), 0)
-        nc.scalar.dma_start(
-            xw[:].bitcast(I32), x_words[0].rearrange("p c r -> p (c r)").bitcast(I32)
+        nc.vector.memset(w1s[:].bitcast(I32), 0)
+        w1s_rows = w1_scales[0].bitcast(I32)
+
+        def load_w1_scales(q):
+            nc.sync.dma_start(
+                w1s[:].bitcast(I32)[32 * q : 32 * q + 4, :], w1s_rows[4 * q : 4 * q + 4, :]
+            )
+
+        nc.sync.dma_start(w1w[:].bitcast(I32), w1_words[0].bitcast(I32))
+        nc.sync.dma_start(
+            xs[:].bitcast(I32), x_scales[0].bitcast(I32).unsqueeze(1).to_broadcast([16, 8, T // 4])
         )
         nc.sync.dma_start(offs_t[:], offs)
         nc.sync.dma_start(cand_t[:], cand)
-        nc.sync.dma_start(xs[:].bitcast(I32)[0:P:8, :], x_scales[0].bitcast(I32))
-        nc.sync.dma_start(w1w[:].bitcast(I32), w1_words[0].bitcast(I32))
+        nc.sync.dma_start(gs_t[:], gs.rearrange("(p t) o -> p (t o)", t=PACK))
+        load_w1_scales(0)
+        load_w1_scales(1)
+        nc.sync.dma_start(
+            xw[:].bitcast(I32), x_words[0].rearrange("p c r -> p (c r)").bitcast(I32)
+        )
+        load_w1_scales(2)
+        load_w1_scales(3)
         nc.vector.memset(warm[:], 0.0)
         nc.scalar.activation(warm_out[:], warm[:], ACT.Tanh)
-        nc.vector.memset(w1s[:].bitcast(I32), 0)
         nc.vector.memset(q_plane[:].bitcast(I32), 0)
-        nc.vector.memset(c_moved[:].bitcast(I32), 0)
-        w1s_rows = w1_scales[0].bitcast(I32)
-        for q in range(4):
-            nc.scalar.dma_start(
-                w1s[:].bitcast(I32)[32 * q : 32 * q + 4, :], w1s_rows[4 * q : 4 * q + 4, :]
-            )
-        make_identity(nc, ident[:])
+        nc.vector.memset(c_plane[:].bitcast(I32), 0)
+        nc.vector.tensor_copy(
+            w1w_dealt[:].rearrange("p (t m b) -> p t m b", t=PACK, b=2),
+            w1w[:].rearrange("p (m t b) -> p t m b", t=PACK, b=2),
+        )
 
         def move_rows(dst, src, queue):
             for r in range(4):
                 queue.dma_start(dst[:].bitcast(I32)[r:P:32, :], src[:].bitcast(I32)[8 * r : P : 32, :])
 
         nc.vector.tensor_copy(q_raw[:], xs[:].indirect(offs_t[:]))
-        move_rows(q_plane, q_raw, nc.sync)
+        move_rows(q_plane, q_raw, nc.scalar)
         nc.vector.tensor_copy(c_raw[:], xs[:].indirect(cand_t[:]))
-        move_rows(c_moved, c_raw, nc.sync)
-        nc.sync.dma_start(gs_t[:], gs.rearrange("(p t) o -> p (t o)", t=PACK))
+        nc.vector.tensor_copy(
+            c_dealt[:].rearrange("p (t m) -> p t m", t=PACK),
+            c_raw[:].rearrange("p (m t) -> p t m", t=PACK),
+        )
+        move_rows(c_plane, c_dealt, nc.sync)
+        nc.vector.tensor_copy(
+            w1s_dealt[:].rearrange("p (t m) -> p t m", t=PACK),
+            w1s[:].rearrange("p (m t) -> p t m", t=PACK),
+        )
         nc.vector.tensor_copy(q_words[:], xw[:].indirect(offs_t[:]))
         nc.vector.tensor_copy(c_words_raw[:], xw[:].indirect(cand_t[:]))
         nc.vector.tensor_copy(
             c_words[:].bitcast(I32).rearrange("p (t m) -> p m t", t=PACK),
             c_words_raw[:].bitcast(I32).rearrange("p (m t) -> p m t", t=PACK),
         )
-        nc.vector.tensor_copy(
-            c_plane[:].rearrange("p (t m) -> p t m", t=PACK),
-            c_moved[:].rearrange("p (m t) -> p t m", t=PACK),
-        )
 
         cols = [slice(c * CHUNK, (c + 1) * CHUNK) for c in range(CHUNKS)]
         out_rows = out_0.rearrange("(p t) j -> p t j", t=PACK)
         out_words = out_1[0].rearrange("p c r -> p (c r)").bitcast(I32)
 
-        turned = []
+        h = []
         for c in range(CHUNKS):
-            acc = psum_a.tile([P, H], F32, name="acc", tag="acc")
-            nc.tensor.matmul_mx(
-                out=acc[:],
-                lhsT=q_words[:, cols[c]].bitcast(FP8X4),
-                lhsT_scale=q_plane[:, cols[c]],
-                rhs=w1w[:].bitcast(FP4X4),
-                rhs_scale=w1s[:],
-                start=True,
-                stop=True,
-            )
-            h = keep.tile([P, PACK, P], F32, name="h%d" % c, align_bytes=64)
-            nc.scalar.activation(h[:], acc[:].rearrange("p (m t) -> p t m", t=PACK), ACT.Tanh)
-            tr = psum_t.tile([P, PACK, CHUNK], F32, name="tr", tag="tr")
+            acc = psum_a.tile([P, PACK, CHUNK], F32, name="acc", tag="acc")
             for t in range(PACK):
-                nc.tensor.transpose(tr[:, t, :], h[:, t, :], ident[:])
-            turned.append(tr)
+                nc.tensor.matmul_mx(
+                    out=acc[:, t, :],
+                    lhsT=w1w_dealt[:, 2 * t * P : 2 * (t + 1) * P].bitcast(FP4X4),
+                    lhsT_scale=w1s_dealt[:, t * P : (t + 1) * P],
+                    rhs=q_words[:, cols[c]].bitcast(FP8X4),
+                    rhs_scale=q_plane[:, cols[c]],
+                    start=True,
+                    stop=True,
+                )
+            hc = keep.tile([P, CHUNK, PACK], F32, name="h%d" % c, align_bytes=64)
+            nc.scalar.activation(hc[:], acc[:].rearrange("p t n -> p n t"), ACT.Tanh)
+            h.append(hc)
 
         gs_b = gs_t[:].unsqueeze(1).to_broadcast([P, CHUNK, PACK])
         z = [keep.tile([P, CHUNK, PACK], BF16, name="z%d" % c, align_bytes=64) for c in range(CHUNKS)]
@@ -125,13 +137,13 @@ def tile_picked_candhash_tanh_po_kernel(
         ob = [keep.tile([P, CHUNK, PACK], BF16, name="ob%d" % c, align_bytes=64) for c in range(CHUNKS)]
 
         def weigh(c):
-            nc.vector.tensor_tensor(z[c][:], turned[c][:].rearrange("p t n -> p n t"), gs_b, MULT)
+            nc.vector.tensor_tensor(z[c][:], h[c][:], gs_b, MULT)
 
         def score(c):
             nc.vector.quantize_mx(
                 out=zw[c][:].bitcast(FP8X4), scales=zs[c][:], in_=z[c][:].rearrange("p n t -> p (n t)")
             )
-            acc = psum_a.tile([P, PACK, CHUNK], F32, name="acc2", tag="acc")
+            acc = psum_o.tile([P, PACK, CHUNK], F32, name="acc2", tag="acc2")
             for t in range(PACK):
                 rows = slice(t * P, (t + 1) * P)
                 nc.tensor.matmul_mx(
@@ -155,7 +167,9 @@ def tile_picked_candhash_tanh_po_kernel(
                 scales=o_scales[:, cols[c]],
                 in_=ob[c][:].rearrange("p n t -> p (n t)"),
             )
-            nc.sync.dma_start(out_words[:, cols[c]], o_words[:, cols[c]].bitcast(I32))
+            if c >= CHUNKS - 2:
+                span = slice(0, (c + 1) * CHUNK) if c == CHUNKS - 2 else cols[c]
+                nc.sync.dma_start(out_words[:, span], o_words[:, span].bitcast(I32))
 
         for step in range(CHUNKS + 4):
             if step < CHUNKS:

@@ -18,8 +18,14 @@ MULT = mybir.AluOpType.mult
 
 P = 128
 PACK = 4
+QUADRANT = 32
+QUADRANTS = P // QUADRANT
+ROWS = 4
+BLOCK_PARTITIONS = 8
+LIST_GROUP = 16
 CHUNK = 128
 CHUNKS = S // CHUNK
+OUT_SCALE = 0.0625
 
 
 def tile_picked_candhash_tanh_po_kernel(
@@ -29,18 +35,18 @@ def tile_picked_candhash_tanh_po_kernel(
     with ExitStack() as ctx:
         keep = ctx.enter_context(tc.tile_pool(name="keep", bufs=1))
         shared = ctx.enter_context(tc.tile_pool(name="shared", bufs=1))
-        psum_a = ctx.enter_context(tc.psum_pool(name="psum_a", bufs=4))
-        psum_o = ctx.enter_context(tc.psum_pool(name="psum_o", bufs=4))
+        psum_a = ctx.enter_context(tc.psum_pool(name="psum_a", bufs=CHUNKS))
+        psum_o = ctx.enter_context(tc.psum_pool(name="psum_o", bufs=CHUNKS))
 
-        offs_t = keep.tile([P, S // 16], U16, name="offs_t")
-        cand_t = keep.tile([P, V // 16], U16, name="cand_t")
+        offs_t = keep.tile([P, S // LIST_GROUP], U16, name="offs_t")
+        cand_t = keep.tile([P, V // LIST_GROUP], U16, name="cand_t")
         xw = keep.tile([P, T], U32, name="xw", align_bytes=64)
-        xs = shared.tile([P, T], U8, name="xs", align_bytes=64, offset=1024)
+        xs = shared.tile([P, T], U8, name="xs", align_bytes=64, offset=T // 2)
         w1w = keep.tile([P, 2 * H], U8, name="w1w", align_bytes=64)
-        w1s = shared.tile([P, H], U8, name="w1s", align_bytes=64, offset=3072)
+        w1s = shared.tile([P, H], U8, name="w1s", align_bytes=64, offset=T // 2 + T)
         gs_t = keep.tile([P, PACK], F32, name="gs_t", align_bytes=64)
         q_words = shared.tile([P, S], U32, name="q_words", align_bytes=64, offset=0)
-        c_words_raw = shared.tile([P, V], U32, name="c_words_raw", align_bytes=64, offset=2048)
+        c_words_raw = shared.tile([P, V], U32, name="c_words_raw", align_bytes=64, offset=4 * S)
         q_raw = keep.tile([P, S], U8, name="q_raw", align_bytes=64)
         q_plane = keep.tile([P, S], U8, name="q_plane", align_bytes=64)
         c_raw = keep.tile([P, V], U8, name="c_raw", align_bytes=64)
@@ -49,58 +55,55 @@ def tile_picked_candhash_tanh_po_kernel(
         c_plane = keep.tile([P, V], U8, name="c_plane", align_bytes=64)
         w1w_dealt = keep.tile([P, 2 * H], U8, name="w1w_dealt", align_bytes=64)
         w1s_dealt = keep.tile([P, H], U8, name="w1s_dealt", align_bytes=64)
-        warm = keep.tile([P, 8], F32, name="warm", align_bytes=64)
-        warm_out = keep.tile([P, 8], F32, name="warm_out", align_bytes=64)
         o_words = keep.tile([P, S], U32, name="o_words", align_bytes=64)
         o_scales = keep.tile([P, S], U8, name="o_scales", align_bytes=64)
 
+        nc.vector.memset(xs[:].bitcast(I32), 0)
         nc.vector.memset(w1s[:].bitcast(I32), 0)
         w1s_rows = w1_scales[0].bitcast(I32)
 
         def load_w1_scales(q):
             nc.sync.dma_start(
-                w1s[:].bitcast(I32)[32 * q : 32 * q + 4, :], w1s_rows[4 * q : 4 * q + 4, :]
+                w1s[:].bitcast(I32)[QUADRANT * q : QUADRANT * q + ROWS, :],
+                w1s_rows[ROWS * q : ROWS * (q + 1), :],
             )
 
         nc.sync.dma_start(w1w[:].bitcast(I32), w1_words[0].bitcast(I32))
-        nc.sync.dma_start(
-            xs[:].bitcast(I32), x_scales[0].bitcast(I32).unsqueeze(1).to_broadcast([16, 8, T // 4])
-        )
         nc.sync.dma_start(offs_t[:], offs)
         nc.sync.dma_start(cand_t[:], cand)
         nc.sync.dma_start(gs_t[:], gs.rearrange("(p t) o -> p (t o)", t=PACK))
-        load_w1_scales(0)
-        load_w1_scales(1)
-        nc.sync.dma_start(
-            xw[:].bitcast(I32), x_words[0].rearrange("p c r -> p (c r)").bitcast(I32)
-        )
-        load_w1_scales(2)
-        load_w1_scales(3)
-        nc.vector.memset(warm[:], 0.0)
-        nc.scalar.activation(warm_out[:], warm[:], ACT.Tanh)
+        nc.sync.dma_start(xs[:].bitcast(I32)[0:P:BLOCK_PARTITIONS, :], x_scales[0].bitcast(I32))
+        for q in range(QUADRANTS // 2):
+            load_w1_scales(q)
+        nc.sync.dma_start(xw[:].bitcast(I32), x_words[0].rearrange("p c r -> p (c r)").bitcast(I32))
+        for q in range(QUADRANTS // 2, QUADRANTS):
+            load_w1_scales(q)
         nc.vector.memset(q_plane[:].bitcast(I32), 0)
         nc.vector.memset(c_plane[:].bitcast(I32), 0)
+
         nc.vector.tensor_copy(
             w1w_dealt[:].rearrange("p (t m b) -> p t m b", t=PACK, b=2),
             w1w[:].rearrange("p (m t b) -> p t m b", t=PACK, b=2),
         )
 
-        def move_rows(dst, src, queue):
-            for r in range(4):
-                queue.dma_start(dst[:].bitcast(I32)[r:P:32, :], src[:].bitcast(I32)[8 * r : P : 32, :])
+        def deal_bytes(dst, src):
+            nc.vector.tensor_copy(
+                dst[:].rearrange("p (t m) -> p t m", t=PACK), src[:].rearrange("p (m t) -> p t m", t=PACK)
+            )
+
+        def move_rows(plane, src, queue):
+            for r in range(ROWS):
+                queue.dma_start(
+                    plane[:].bitcast(I32)[r:P:QUADRANT, :],
+                    src[:].bitcast(I32)[BLOCK_PARTITIONS * r : P : QUADRANT, :],
+                )
 
         nc.vector.tensor_copy(q_raw[:], xs[:].indirect(offs_t[:]))
         move_rows(q_plane, q_raw, nc.scalar)
         nc.vector.tensor_copy(c_raw[:], xs[:].indirect(cand_t[:]))
-        nc.vector.tensor_copy(
-            c_dealt[:].rearrange("p (t m) -> p t m", t=PACK),
-            c_raw[:].rearrange("p (m t) -> p t m", t=PACK),
-        )
+        deal_bytes(c_dealt, c_raw)
         move_rows(c_plane, c_dealt, nc.sync)
-        nc.vector.tensor_copy(
-            w1s_dealt[:].rearrange("p (t m) -> p t m", t=PACK),
-            w1s[:].rearrange("p (m t) -> p t m", t=PACK),
-        )
+        deal_bytes(w1s_dealt, w1s)
         nc.vector.tensor_copy(q_words[:], xw[:].indirect(offs_t[:]))
         nc.vector.tensor_copy(c_words_raw[:], xw[:].indirect(cand_t[:]))
         nc.vector.tensor_copy(
@@ -125,63 +128,73 @@ def tile_picked_candhash_tanh_po_kernel(
                     start=True,
                     stop=True,
                 )
-            hc = keep.tile([P, CHUNK, PACK], F32, name="h%d" % c, align_bytes=64)
-            nc.scalar.activation(hc[:], acc[:].rearrange("p t n -> p n t"), ACT.Tanh)
-            h.append(hc)
+            h_c = keep.tile([P, CHUNK, PACK], F32, name="h%d" % c, align_bytes=64)
+            nc.scalar.activation(h_c[:], acc[:].rearrange("p t n -> p n t"), ACT.Tanh)
+            h.append(h_c)
 
         gs_b = gs_t[:].unsqueeze(1).to_broadcast([P, CHUNK, PACK])
         z = [keep.tile([P, CHUNK, PACK], BF16, name="z%d" % c, align_bytes=64) for c in range(CHUNKS)]
-        zw = [keep.tile([P, CHUNK], U32, name="zw%d" % c, align_bytes=64) for c in range(CHUNKS)]
-        zs = [keep.tile([P, CHUNK], U8, name="zs%d" % c, align_bytes=64) for c in range(CHUNKS)]
+        z_words = [keep.tile([P, CHUNK], U32, name="zw%d" % c, align_bytes=64) for c in range(CHUNKS)]
+        z_scales = [keep.tile([P, CHUNK], U8, name="zs%d" % c, align_bytes=64) for c in range(CHUNKS)]
         o32 = [keep.tile([P, PACK, CHUNK], F32, name="o32_%d" % c, align_bytes=64) for c in range(CHUNKS)]
-        ob = [keep.tile([P, CHUNK, PACK], BF16, name="ob%d" % c, align_bytes=64) for c in range(CHUNKS)]
+        o16 = [keep.tile([P, CHUNK, PACK], BF16, name="ob%d" % c, align_bytes=64) for c in range(CHUNKS)]
 
         def weigh(c):
             nc.vector.tensor_tensor(z[c][:], h[c][:], gs_b, MULT)
 
         def score(c):
             nc.vector.quantize_mx(
-                out=zw[c][:].bitcast(FP8X4), scales=zs[c][:], in_=z[c][:].rearrange("p n t -> p (n t)")
+                out=z_words[c][:].bitcast(FP8X4),
+                scales=z_scales[c][:],
+                in_=z[c][:].rearrange("p n t -> p (n t)"),
             )
-            acc = psum_o.tile([P, PACK, CHUNK], F32, name="acc2", tag="acc2")
+            scores = psum_o.tile([P, PACK, CHUNK], F32, name="acc2", tag="acc2")
             for t in range(PACK):
                 rows = slice(t * P, (t + 1) * P)
                 nc.tensor.matmul_mx(
-                    out=acc[:, t, :],
+                    out=scores[:, t, :],
                     lhsT=c_words[:, rows].bitcast(FP8X4),
                     lhsT_scale=c_plane[:, rows],
-                    rhs=zw[c][:].bitcast(FP8X4),
-                    rhs_scale=zs[c][:],
+                    rhs=z_words[c][:].bitcast(FP8X4),
+                    rhs_scale=z_scales[c][:],
                     start=True,
                     stop=True,
                 )
-            nc.scalar.activation(o32[c][:], acc[:], ACT.Copy, scale=0.0625)
+            nc.scalar.activation(o32[c][:], scores[:], ACT.Copy, scale=OUT_SCALE)
             nc.sync.dma_start(out_rows[:, :, cols[c]], o32[c][:])
 
         def round_out(c):
-            nc.vector.tensor_copy(ob[c][:], o32[c][:].rearrange("p t n -> p n t"))
+            nc.vector.tensor_copy(o16[c][:], o32[c][:].rearrange("p t n -> p n t"))
 
         def pack_out(c):
             nc.vector.quantize_mx(
                 out=o_words[:, cols[c]].bitcast(FP8X4),
                 scales=o_scales[:, cols[c]],
-                in_=ob[c][:].rearrange("p n t -> p (n t)"),
+                in_=o16[c][:].rearrange("p n t -> p (n t)"),
             )
-            if c >= CHUNKS - 2:
-                span = slice(0, (c + 1) * CHUNK) if c == CHUNKS - 2 else cols[c]
-                nc.sync.dma_start(out_words[:, span], o_words[:, span].bitcast(I32))
 
-        for step in range(CHUNKS + 4):
+        def store_words(span):
+            nc.sync.dma_start(out_words[:, span], o_words[:, span].bitcast(I32))
+
+        score_lag, round_lag, pack_lag = 1, 3, 4
+        last = CHUNKS - 1
+        for step in range(CHUNKS + pack_lag):
             if step < CHUNKS:
                 weigh(step)
-            if 0 <= step - 1 < CHUNKS:
-                score(step - 1)
-            if 0 <= step - 3 < CHUNKS:
-                round_out(step - 3)
-            if 0 <= step - 4 < CHUNKS:
-                pack_out(step - 4)
+            if 0 <= step - score_lag < CHUNKS:
+                score(step - score_lag)
+            if 0 <= step - round_lag < CHUNKS:
+                round_out(step - round_lag)
+            if 0 <= step - pack_lag < CHUNKS:
+                pack_out(step - pack_lag)
+            if step - pack_lag == last - 1:
+                store_words(slice(0, last * CHUNK))
+        store_words(cols[last])
 
         scale_rows = out_2[0].bitcast(I32)
-        for q in range(4):
+        for q in range(QUADRANTS):
             queue = nc.sync if q % 2 == 0 else nc.scalar
-            queue.dma_start(scale_rows[4 * q : 4 * q + 4, :], o_scales[:].bitcast(I32)[32 * q : 32 * q + 4, :])
+            queue.dma_start(
+                scale_rows[ROWS * q : ROWS * (q + 1), :],
+                o_scales[:].bitcast(I32)[QUADRANT * q : QUADRANT * q + ROWS, :],
+            )

@@ -162,6 +162,10 @@ def tile_picked_candhash_tanh_po_kernel(
                 )
             nc.scalar.activation(o32[c][:], scores[:], ACT.Copy, scale=OUT_SCALE)
             nc.sync.dma_start(out_rows[:, :, cols[c]], o32[c][:])
+            if c == CHUNKS - 1:
+                nc.scalar.activation(
+                    o16[c][:], scores[:].rearrange("p t n -> p n t"), ACT.Copy, scale=OUT_SCALE
+                )
 
         def round_out(c):
             nc.vector.tensor_copy(o16[c][:], o32[c][:].rearrange("p t n -> p n t"))
@@ -183,7 +187,7 @@ def tile_picked_candhash_tanh_po_kernel(
                 weigh(step)
             if 0 <= step - score_lag < CHUNKS:
                 score(step - score_lag)
-            if 0 <= step - round_lag < CHUNKS:
+            if 0 <= step - round_lag < last:
                 round_out(step - round_lag)
             if 0 <= step - pack_lag < CHUNKS:
                 pack_out(step - pack_lag)

from contextlib import ExitStack

import concourse.mybir as mybir

K, T, S, V, H = 512, 2048, 512, 512, 512
FLOPS = 2 * K * H * S + 2 * K * V * S

F32 = mybir.dt.float32
BF16 = mybir.dt.bfloat16
I32 = mybir.dt.int32
U32 = mybir.dt.uint32
U16 = mybir.dt.uint16
U8 = mybir.dt.uint8
FP8X4 = mybir.dt.float8_e4m3fn_x4
FP4X4 = mybir.dt.float4_e2m1fn_x4
ACT = mybir.ActivationFunctionType
MULT = mybir.AluOpType.mult

P = 128
PACK = 4
QUADRANT = 32
QUADRANTS = P // QUADRANT
ROWS = 4
BLOCK_PARTITIONS = 8
LIST_GROUP = 16
CHUNK = 128
CHUNKS = S // CHUNK
OUT_SCALE = 0.0625


def tile_picked_candhash_tanh_po_kernel(
    tc, x_words, x_scales, w1_words, w1_scales, gs, offs, cand, out_0, out_1, out_2
):
    nc = tc.nc
    with ExitStack() as ctx:
        keep = ctx.enter_context(tc.tile_pool(name="keep", bufs=1))
        shared = ctx.enter_context(tc.tile_pool(name="shared", bufs=1))
        psum_a = ctx.enter_context(tc.psum_pool(name="psum_a", bufs=CHUNKS))
        psum_o = ctx.enter_context(tc.psum_pool(name="psum_o", bufs=CHUNKS))

        offs_t = keep.tile([P, S // LIST_GROUP], U16, name="offs_t")
        cand_t = keep.tile([P, V // LIST_GROUP], U16, name="cand_t")
        xw = keep.tile([P, T], U32, name="xw", align_bytes=64)
        xs = shared.tile([P, T], U8, name="xs", align_bytes=64, offset=T // 2)
        w1w = keep.tile([P, 2 * H], U8, name="w1w", align_bytes=64)
        w1s = shared.tile([P, H], U8, name="w1s", align_bytes=64, offset=T // 2 + T)
        gs_t = keep.tile([P, PACK], F32, name="gs_t", align_bytes=64)
        q_words = shared.tile([P, S], U32, name="q_words", align_bytes=64, offset=0)
        c_words_raw = shared.tile([P, V], U32, name="c_words_raw", align_bytes=64, offset=4 * S)
        q_raw = keep.tile([P, S], U8, name="q_raw", align_bytes=64)
        q_plane = keep.tile([P, S], U8, name="q_plane", align_bytes=64)
        c_raw = keep.tile([P, V], U8, name="c_raw", align_bytes=64)
        c_dealt = keep.tile([P, V], U8, name="c_dealt", align_bytes=64)
        c_words = keep.tile([P, V], U32, name="c_words", align_bytes=64)
        c_plane = keep.tile([P, V], U8, name="c_plane", align_bytes=64)
        w1w_dealt = keep.tile([P, 2 * H], U8, name="w1w_dealt", align_bytes=64)
        w1s_dealt = keep.tile([P, H], U8, name="w1s_dealt", align_bytes=64)
        o_words = keep.tile([P, S], U32, name="o_words", align_bytes=64)
        o_scales = keep.tile([P, S], U8, name="o_scales", align_bytes=64)

        nc.vector.memset(xs[:].bitcast(I32), 0)
        nc.vector.memset(w1s[:].bitcast(I32), 0)
        w1s_rows = w1_scales[0].bitcast(I32)

        def load_w1_scales(q):
            nc.sync.dma_start(
                w1s[:].bitcast(I32)[QUADRANT * q : QUADRANT * q + ROWS, :],
                w1s_rows[ROWS * q : ROWS * (q + 1), :],
            )

        nc.sync.dma_start(w1w[:].bitcast(I32), w1_words[0].bitcast(I32))
        nc.sync.dma_start(offs_t[:], offs)
        nc.sync.dma_start(cand_t[:], cand)
        nc.sync.dma_start(gs_t[:], gs.rearrange("(p t) o -> p (t o)", t=PACK))
        nc.sync.dma_start(xs[:].bitcast(I32)[0:P:BLOCK_PARTITIONS, :], x_scales[0].bitcast(I32))
        for q in range(QUADRANTS // 2):
            load_w1_scales(q)
        nc.sync.dma_start(xw[:].bitcast(I32), x_words[0].rearrange("p c r -> p (c r)").bitcast(I32))
        for q in range(QUADRANTS // 2, QUADRANTS):
            load_w1_scales(q)
        nc.vector.memset(q_plane[:].bitcast(I32), 0)
        nc.vector.memset(c_plane[:].bitcast(I32), 0)

        nc.vector.tensor_copy(
            w1w_dealt[:].rearrange("p (t m b) -> p t m b", t=PACK, b=2),
            w1w[:].rearrange("p (m t b) -> p t m b", t=PACK, b=2),
        )

        def deal_bytes(dst, src):
            nc.vector.tensor_copy(
                dst[:].rearrange("p (t m) -> p t m", t=PACK), src[:].rearrange("p (m t) -> p t m", t=PACK)
            )

        def move_rows(plane, src, queue):
            for r in range(ROWS):
                queue.dma_start(
                    plane[:].bitcast(I32)[r:P:QUADRANT, :],
                    src[:].bitcast(I32)[BLOCK_PARTITIONS * r : P : QUADRANT, :],
                )

        nc.vector.tensor_copy(q_raw[:], xs[:].indirect(offs_t[:]))
        move_rows(q_plane, q_raw, nc.scalar)
        nc.vector.tensor_copy(c_raw[:], xs[:].indirect(cand_t[:]))
        deal_bytes(c_dealt, c_raw)
        move_rows(c_plane, c_dealt, nc.sync)
        deal_bytes(w1s_dealt, w1s)
        nc.vector.tensor_copy(q_words[:], xw[:].indirect(offs_t[:]))
        nc.vector.tensor_copy(c_words_raw[:], xw[:].indirect(cand_t[:]))
        nc.vector.tensor_copy(
            c_words[:].bitcast(I32).rearrange("p (t m) -> p m t", t=PACK),
            c_words_raw[:].bitcast(I32).rearrange("p (m t) -> p m t", t=PACK),
        )

        cols = [slice(c * CHUNK, (c + 1) * CHUNK) for c in range(CHUNKS)]
        out_rows = out_0.rearrange("(p t) j -> p t j", t=PACK)
        out_words = out_1[0].rearrange("p c r -> p (c r)").bitcast(I32)

        h = []
        for c in range(CHUNKS):
            acc = psum_a.tile([P, PACK, CHUNK], F32, name="acc", tag="acc")
            for t in range(PACK):
                nc.tensor.matmul_mx(
                    out=acc[:, t, :],
                    lhsT=w1w_dealt[:, 2 * t * P : 2 * (t + 1) * P].bitcast(FP4X4),
                    lhsT_scale=w1s_dealt[:, t * P : (t + 1) * P],
                    rhs=q_words[:, cols[c]].bitcast(FP8X4),
                    rhs_scale=q_plane[:, cols[c]],
                    start=True,
                    stop=True,
                )
            h_c = keep.tile([P, CHUNK, PACK], F32, name="h%d" % c, align_bytes=64)
            nc.scalar.activation(h_c[:], acc[:].rearrange("p t n -> p n t"), ACT.Tanh)
            h.append(h_c)

        gs_b = gs_t[:].unsqueeze(1).to_broadcast([P, CHUNK, PACK])
        z = [keep.tile([P, CHUNK, PACK], BF16, name="z%d" % c, align_bytes=64) for c in range(CHUNKS)]
        z_words = [keep.tile([P, CHUNK], U32, name="zw%d" % c, align_bytes=64) for c in range(CHUNKS)]
        z_scales = [keep.tile([P, CHUNK], U8, name="zs%d" % c, align_bytes=64) for c in range(CHUNKS)]
        o32 = [keep.tile([P, PACK, CHUNK], F32, name="o32_%d" % c, align_bytes=64) for c in range(CHUNKS)]
        o16 = [keep.tile([P, CHUNK, PACK], BF16, name="ob%d" % c, align_bytes=64) for c in range(CHUNKS)]

        def weigh(c):
            nc.vector.tensor_tensor(z[c][:], h[c][:], gs_b, MULT)

        def score(c):
            nc.vector.quantize_mx(
                out=z_words[c][:].bitcast(FP8X4),
                scales=z_scales[c][:],
                in_=z[c][:].rearrange("p n t -> p (n t)"),
            )
            scores = psum_o.tile([P, PACK, CHUNK], F32, name="acc2", tag="acc2")
            for t in range(PACK):
                rows = slice(t * P, (t + 1) * P)
                nc.tensor.matmul_mx(
                    out=scores[:, t, :],
                    lhsT=c_words[:, rows].bitcast(FP8X4),
                    lhsT_scale=c_plane[:, rows],
                    rhs=z_words[c][:].bitcast(FP8X4),
                    rhs_scale=z_scales[c][:],
                    start=True,
                    stop=True,
                )
            nc.scalar.activation(o32[c][:], scores[:], ACT.Copy, scale=OUT_SCALE)
            nc.sync.dma_start(out_rows[:, :, cols[c]], o32[c][:])
            if c == CHUNKS - 1:
                nc.scalar.activation(
                    o16[c][:], scores[:].rearrange("p t n -> p n t"), ACT.Copy, scale=OUT_SCALE
                )

        def round_out(c):
            nc.vector.tensor_copy(o16[c][:], o32[c][:].rearrange("p t n -> p n t"))

        def pack_out(c):
            nc.vector.quantize_mx(
                out=o_words[:, cols[c]].bitcast(FP8X4),
                scales=o_scales[:, cols[c]],
                in_=o16[c][:].rearrange("p n t -> p (n t)"),
            )

        def store_words(span):
            nc.sync.dma_start(out_words[:, span], o_words[:, span].bitcast(I32))

        score_lag, round_lag, pack_lag = 1, 3, 4
        last = CHUNKS - 1
        for step in range(CHUNKS + pack_lag):
            if step < CHUNKS:
                weigh(step)
            if 0 <= step - score_lag < CHUNKS:
                score(step - score_lag)
            if 0 <= step - round_lag < last:
                round_out(step - round_lag)
            if 0 <= step - pack_lag < CHUNKS:
                pack_out(step - pack_lag)
            if step - pack_lag == last - 1:
                store_words(slice(0, last * CHUNK))
        store_words(cols[last])

        scale_rows = out_2[0].bitcast(I32)
        for q in range(QUADRANTS):
            queue = nc.sync if q % 2 == 0 else nc.scalar
            queue.dma_start(
                scale_rows[ROWS * q : ROWS * (q + 1), :],
                o_scales[:].bitcast(I32)[QUADRANT * q : QUADRANT * q + ROWS, :],
            )
